import numpy as np
import ml_dtypes


def mxq(x, axis, fmt="e4m3"):
    dtype, down = {"e4m3": (ml_dtypes.float8_e4m3fn, 7), "e5m2": (ml_dtypes.float8_e5m2, 14)}[fmt]
    v = np.moveaxis(np.asarray(x, np.float32).astype(ml_dtypes.bfloat16).astype(np.float64), axis, -1)
    blocks = v.reshape(v.shape[:-1] + (-1, 32))
    amax = np.abs(blocks).max(-1, keepdims=True)
    byte = np.maximum(np.where(amax > 0, np.frexp(amax)[1] - 1 + 127, 0) - down, 1)
    scale = np.exp2(byte - 127.0)
    codes = (blocks / scale).astype(np.float32).astype(dtype).astype(np.float64)
    return np.moveaxis((codes * scale).reshape(v.shape), -1, axis)


WIDE = False


def mx_kscale(k):
    if not WIDE:
        return np.ones(k)
    levels = np.array([10, -10, 5, -5, 0])
    if k % 512:
        return np.exp2(np.random.permutation(np.resize(levels, k // 32))).repeat(32)
    a = np.empty((k // 512, 16))
    for p in range(k // 512):
        a[p, :8] = np.random.permutation(np.resize(levels, 8))
        for g in range(8):
            far = levels[np.abs(levels - a[p, g]) >= 10]
            a[p, g + 8] = far[np.random.randint(len(far))]
    return np.exp2(a.ravel()).repeat(32)


def f64(x):
    return np.asarray(x).astype(np.float64)


def striped(idx):
    return np.tile(np.asarray(idx).reshape(-1, 16).T, (8, 1)).astype(np.uint16)


def unstriped(offs):
    return offs[:16].T.reshape(-1).astype(np.int64)


def striped8(idx):
    return np.asarray(idx).reshape(8, -1, 16).transpose(0, 2, 1).reshape(128, -1).astype(np.uint16)


def unstriped8(offs):
    return offs.reshape(8, 16, -1).transpose(0, 2, 1).reshape(8, -1).astype(np.int64)


def pick8(x, idx, run):
    r = np.arange(len(x))
    return x[r[:, None], idx[r % (8 * run) // run]]


E2M1 = np.array([0.0, 0.5, 1.0, 1.5, 2.0, 3.0, 4.0, 6.0, -0.0, -0.5, -1.0, -1.5, -2.0, -3.0, -4.0, -6.0])


def pack_weight(w, fmt):
    k, n = w.shape
    w = f64(np.asarray(w, np.float32).astype(ml_dtypes.bfloat16)).reshape(k // 32, 32, n)
    amax = np.abs(w).max(1)
    if fmt == "e4m3":
        byte = np.frexp(amax)[1] - 1 + 127 - 7
    else:
        mant, ex = np.frexp(amax / 6.0)
        byte = np.where(mant > 0.5, ex, ex - 1) + 127
    byte = np.clip(np.where(amax > 0, byte, 1), 1, 254)
    scaled = (w * np.exp2(127.0 - byte)[:, None, :]).reshape(k, n).astype(np.float32)
    by_word = np.ascontiguousarray(scaled.reshape(k // 512, 128, 4, n).transpose(0, 1, 3, 2))
    if fmt == "e4m3":
        words = by_word.astype(ml_dtypes.float8_e4m3fn).view(np.uint8)
    else:
        c = by_word.astype(ml_dtypes.float4_e2m1fn).view(np.uint8) & 0xF
        words = (c[..., 0::2] | (c[..., 1::2] << 4)).reshape(k // 512, 128, 2 * n)
    return np.ascontiguousarray(words), np.ascontiguousarray(byte.astype(np.uint8).reshape(k // 512, 16, n))


def unpack_weight(words, scales, fmt):
    g, _, n = scales.shape
    words = np.ascontiguousarray(words).reshape(g, 128, n, -1)
    if fmt == "e4m3":
        vals = words.view(ml_dtypes.float8_e4m3fn).astype(np.float64)
    else:
        nib = np.empty((g, 128, n, 4), np.uint8)
        nib[..., 0::2] = words & 0xF
        nib[..., 1::2] = words >> 4
        vals = E2M1[nib]
    vals = vals * np.repeat(np.exp2(scales.astype(np.float64) - 127.0), 8, axis=1)[..., None]
    return vals.transpose(0, 1, 3, 2).reshape(g * 512, n)


K, R, F, T, J, M, G = 512, 128, 512, 2048, 512, 256, 32


def setup_inputs():
    n = np.random.standard_normal
    idx = np.random.permutation(T)[:J]
    idx2 = np.stack([np.random.permutation(J)[:M] for _ in range(8)])
    fk = mx_kscale(K)
    ff = mx_kscale(F)
    tabp = pack_weight(n((K, T)) / fk[:, None], "e4m3")
    return {
        "tab_words": tabp[0],
        "tab_scales": tabp[1],
        "w1": (n((K, R)) * 1 / np.sqrt(K) * fk[:, None]).astype(np.float32),
        "temper": (np.random.uniform(0.5, 1.5, (R, 1))).astype(np.float32),
        "pw": (np.random.uniform(0.5, 1.5, (1, M))).astype(np.float32),
        "wo": (n((F, R)) * 1 / np.sqrt(F) * ff[:, None]).astype(np.float32),
        "dy": (n((F, M)) / ff[:, None]).astype(np.float32),
        "old": (0.5 * n((R, J))).astype(np.float32),
        "offs": striped(idx),
        "offs2": striped8(idx2),
    }


def reference(tab_words, tab_scales, w1, temper, pw, wo, dy, old, offs, offs2):
    idx = unstriped(offs)
    idx2 = unstriped8(offs2)
    tabu = unpack_weight(tab_words, tab_scales, "e4m3")
    w1q = mxq(f64(w1), 0, "e4m3")
    tabidxg = tabu[:, idx]
    a = w1q.T @ tabidxg
    p1 = np.exp(a * f64(temper))
    s = pick8(p1, idx2, 16) * f64(pw)
    z1 = s.reshape(R, G, M // G).sum(axis=2)
    zr = np.repeat(z1, M // G, axis=1)
    woq = mxq(f64(wo), 0, "e4m3")
    dyq = mxq(f64(dy), 0, "e4m3")
    c0 = woq.T @ dyq
    dzr = c0 / (s / zr * 8.0 + 1.0) * 8.0 * s / np.square(zr) * (-1.0)
    dz1 = dzr.reshape(R, G, M // G).sum(axis=2)
    r1 = np.repeat(dz1, M // G, axis=1)
    ds = c0 / (s / zr * 8.0 + 1.0) * 8.0 / zr + r1
    e2 = ds * f64(pw)
    s2 = np.zeros((R, J))
    s2[np.arange(R)[:, None], idx2[np.arange(R) % 128 // 16]] = e2
    da = s2 * p1 * f64(temper)
    y = da + f64(old)
    return y

@@ -1,0 +1,168 @@
+from contextlib import ExitStack
+
+import concourse.mybir as mybir
+from concourse.masks import make_identity
+
+K, R, F, T, J, M, G = 512, 128, 512, 2048, 512, 256, 32
+FLOPS = 2 * K * R * J + 2 * F * R * M
+
+F32 = mybir.dt.float32
+BF16 = mybir.dt.bfloat16
+I32 = mybir.dt.int32
+U32 = mybir.dt.uint32
+U16 = mybir.dt.uint16
+U8 = mybir.dt.uint8
+FP8X4 = mybir.dt.float8_e4m3fn_x4
+ALU = mybir.AluOpType
+ACT = mybir.ActivationFunctionType
+AX = mybir.AxisListType
+
+P = 128
+PACK = 4
+GROUP = M // G
+HALVES = 2
+
+
+def tile_attend_cpickshares_kernel(tc, tab_words, tab_scales, w1, temper, pw, wo, dy, old, offs, offs2, out):
+    nc = tc.nc
+    jh = J // HALVES
+    mh = M // HALVES
+    gh = G // HALVES
+    with ExitStack() as ctx:
+        keep = ctx.enter_context(tc.tile_pool(name="keep", bufs=1))
+        psum = ctx.enter_context(tc.psum_pool(name="psum", bufs=1))
+
+        slots = keep.tile([P, J // 16], U16, name="slots")
+        nc.sync.dma_start(slots[:], offs)
+
+        w1_raw = keep.tile([P, PACK * R], F32, name="w1_raw", align_bytes=64)
+        nc.sync.dma_start(w1_raw[:], w1.rearrange("(p t) r -> p (t r)", t=PACK))
+        tab_plane = keep.tile([P, T], U8, name="tab_plane", align_bytes=64)
+        nc.vector.memset(tab_plane[:].bitcast(I32), 0)
+        scale_rows = tab_scales[0].bitcast(I32)
+        for i in range(PACK):
+            nc.sync.dma_start(tab_plane[:].bitcast(I32)[i:P:32, :], scale_rows[i:16:PACK, :])
+
+        tab_codes = keep.tile([P, T], I32, name="tab_codes", align_bytes=64)
+        nc.sync.dma_start(tab_codes[:], tab_words[0].rearrange("p n t -> p (n t)").bitcast(I32))
+        wo_raw = keep.tile([P, PACK * R], F32, name="wo_raw", tag="wo_then_p1")
+        nc.sync.dma_start(wo_raw[:], wo.rearrange("(p t) r -> p (t r)", t=PACK))
+        dy_raw = keep.tile([P, PACK * M], F32, name="dy_raw", tag="dy_then_s")
+        nc.sync.dma_start(dy_raw[:], dy.rearrange("(p t) m -> p (t m)", t=PACK))
+        picks = keep.tile([P, M // 16], U16, name="picks")
+        nc.sync.dma_start(picks[:], offs2)
+        old_sb = keep.tile([P, J], F32, name="old_sb")
+        nc.sync.dma_start(old_sb[:], old)
+
+        pw_pairs = keep.tile([P, 2], F32, name="pw_pairs")
+        nc.gpsimd.dma_start(pw_pairs[:], pw.rearrange("o (p c) -> (o p) c", c=2))
+        temper_col = keep.tile([P, 1], F32, name="temper_col")
+        nc.gpsimd.dma_start(temper_col[:], temper)
+        ident = keep.tile([P, P], F32, name="ident")
+        make_identity(nc, ident[:])
+        placed = keep.tile([P, J], F32, name="placed")
+        nc.vector.memset(placed[:], 0.0)
+
+        warm = keep.tile([P, 1], F32, name="warm")
+        nc.vector.memset(warm[:], 1.0)
+        warm_exp = keep.tile([P, 1], F32, name="warm_exp")
+        nc.scalar.activation(warm_exp[:], warm[:], ACT.Exp)
+
+        w1_bf = keep.tile([P, R * PACK], BF16, name="w1_bf", align_bytes=64)
+        nc.vector.tensor_copy(w1_bf[:].rearrange("p (r t) -> p r t", t=PACK), w1_raw[:].rearrange("p (t r) -> p r t", t=PACK))
+
+
+        got_plane = keep.tile([P, J], U8, name="got_plane", align_bytes=64)
+        nc.vector.tensor_copy(got_plane[:], tab_plane[:].indirect(slots[:]))
+        w1_codes = keep.tile([P, R], U32, name="w1_codes", align_bytes=64)
+        w1_plane = keep.tile([P, R], U8, name="w1_plane", align_bytes=64)
+        nc.vector.quantize_mx(w1_codes[:].bitcast(FP8X4), w1_plane[:], w1_bf[:])
+        neg_temper = keep.tile([P, 1], F32, name="neg_temper")
+        nc.gpsimd.tensor_scalar(neg_temper[:], temper_col[:], -1.0, 0.0, ALU.mult, ALU.add)
+
+        pw_ps = psum.tile([P, 2, P], F32, name="pw_ps")
+        for c in range(2):
+            nc.tensor.transpose(pw_ps[:, c, :], pw_pairs[:, c : c + 1].to_broadcast([P, P]), ident[:])
+        pw_row = keep.tile([P, M], F32, name="pw_row")
+        nc.scalar.copy(pw_row[:].rearrange("p (q c) -> p q c", c=2), pw_ps[:].rearrange("p c q -> p q c"))
+
+        wo_bf = keep.tile([P, R * PACK], BF16, name="wo_bf", align_bytes=64)
+        nc.scalar.copy(wo_bf[:].rearrange("p (r t) -> p r t", t=PACK), wo_raw[:].rearrange("p (t r) -> p r t", t=PACK))
+
+        p1 = keep.tile([P, J], F32, name="p1", tag="wo_then_p1")
+        for h in range(HALVES):
+            cols = slice(h * jh, (h + 1) * jh)
+            got_codes = keep.tile([P, jh], U32, name="got_codes%d" % h, align_bytes=64)
+            nc.vector.tensor_copy(got_codes[:], tab_codes[:].bitcast(U32).indirect(slots[:, h * jh // 16 : (h + 1) * jh // 16]))
+            a_ps = psum.tile([P, jh], F32, name="a_ps%d" % h)
+            nc.tensor.matmul_mx(a_ps[:], lhsT=w1_codes[:].bitcast(FP8X4), lhsT_scale=w1_plane[:],
+                                rhs=got_codes[:].bitcast(FP8X4), rhs_scale=got_plane[:, cols], start=True, stop=True)
+            nc.scalar.activation(p1[:, cols], a_ps[:], ACT.Exp, scale=temper_col[:])
+        warm_ars = keep.tile([P, 1], F32, name="warm_ars")
+        nc.scalar.activation(warm_ars[:], p1[:, J - 1 : J], ACT.Abs_reciprocal_sqrt)
+
+        wo_codes = keep.tile([P, R], U32, name="wo_codes", align_bytes=64)
+        wo_plane = keep.tile([P, R], U8, name="wo_plane", align_bytes=64)
+        nc.vector.quantize_mx(wo_codes[:].bitcast(FP8X4), wo_plane[:], wo_bf[:])
+        dy_bf = keep.tile([P, M * PACK], BF16, name="dy_bf", align_bytes=64)
+        nc.vector.tensor_copy(dy_bf[:].rearrange("p (m t) -> p m t", t=PACK), dy_raw[:].rearrange("p (t m) -> p m t", t=PACK))
+
+        def half_tiles(name, width):
+            return [keep.tile([P, width], F32, name="%s%d" % (name, h)) for h in range(HALVES)]
+
+        def grouped(tile):
+            return tile[:].rearrange("p (g e) -> p g e", e=GROUP)
+
+        def spread(tile):
+            return tile[:].unsqueeze(2).to_broadcast([P, gh, GROUP])
+
+        def pick_list(h):
+            return picks[:, h * mh // 16 : (h + 1) * mh // 16]
+
+        s_both = keep.tile([P, M], F32, name="s_both", tag="dy_then_s")
+        s = [s_both[:, h * mh : (h + 1) * mh] for h in range(HALVES)]
+        z = half_tiles("z", gh)
+        rz = half_tiles("rz", gh)
+        share = half_tiles("share", mh)
+        root = half_tiles("root", mh)
+        inv = half_tiles("inv", mh)
+        wn = half_tiles("wn", mh)
+        wsum = half_tiles("wsum", gh)
+        back = half_tiles("back", mh)
+        both = range(HALVES)
+
+        for h in both:
+            nc.vector.tensor_tensor(s[h][:], p1[:].indirect(pick_list(h)), pw_row[:, h * mh : (h + 1) * mh], ALU.mult)
+        for h in both:
+            nc.vector.tensor_reduce(z[h][:], grouped(s[h]), AX.X, ALU.add)
+        for h in both:
+            nc.vector.reciprocal(rz[h][:], z[h][:])
+        for h in both:
+            nc.vector.tensor_tensor(grouped(share[h]), grouped(s[h]), spread(rz[h]), ALU.mult)
+        for h in both:
+            nc.scalar.activation(root[h][:], share[h][:], ACT.Abs_reciprocal_sqrt, bias=1.0, scale=8.0)
+        for h in both:
+            nc.scalar.activation(inv[h][:], root[h][:], ACT.Square)
+
+        dy_codes = keep.tile([P, M], U32, name="dy_codes", align_bytes=64)
+        dy_plane = keep.tile([P, M], U8, name="dy_plane", align_bytes=64)
+        nc.vector.quantize_mx(dy_codes[:].bitcast(FP8X4), dy_plane[:], dy_bf[:])
+        c0 = psum.tile([P, M], F32, name="c0")
+        nc.tensor.matmul_mx(c0[:], lhsT=wo_codes[:].bitcast(FP8X4), lhsT_scale=wo_plane[:],
+                            rhs=dy_codes[:].bitcast(FP8X4), rhs_scale=dy_plane[:], start=True, stop=True)
+
+        for h in both:
+            nc.vector.scalar_tensor_tensor(wn[h][:], inv[h][:], 1.0, c0[:, h * mh : (h + 1) * mh], ALU.subtract, ALU.mult)
+        for h in both:
+            nc.vector.tensor_reduce(wsum[h][:], grouped(wn[h]), AX.X, ALU.add)
+        for h in both:
+            nc.vector.scalar_tensor_tensor(grouped(back[h]), grouped(share[h]), -1.0, spread(wsum[h]), ALU.mult, ALU.mult)
+        for h in both:
+            nc.vector.tensor_tensor(placed[:].indirect(pick_list(h)), wn[h][:], back[h][:], ALU.add)
+
+        queues = (nc.sync, nc.scalar)
+        for h in both:
+            cols = slice(h * jh, (h + 1) * jh)
+            result = keep.tile([P, jh], F32, name="result%d" % h)
+            nc.vector.scalar_tensor_tensor(result[:], placed[:, cols], neg_temper[:], old_sb[:, cols], ALU.mult, ALU.add)
+            queues[h].dma_start(out[:, cols], result[:])

@@ -37,6 +37,8 @@ def tile_attend_cpickshares_kernel(tc, tab_words, tab_scales, w1, temper, pw, wo
 
         w1_raw = keep.tile([P, PACK * R], F32, name="w1_raw", align_bytes=64)
         nc.sync.dma_start(w1_raw[:], w1.rearrange("(p t) r -> p (t r)", t=PACK))
+        pw_pairs = keep.tile([P, 2], F32, name="pw_pairs")
+        nc.sync.dma_start(pw_pairs[:], pw.rearrange("o (p c) -> (o p) c", c=2))
         tab_plane = keep.tile([P, T], U8, name="tab_plane", align_bytes=64)
         nc.vector.memset(tab_plane[:].bitcast(I32), 0)
         scale_rows = tab_scales[0].bitcast(I32)
@@ -45,6 +47,8 @@ def tile_attend_cpickshares_kernel(tc, tab_words, tab_scales, w1, temper, pw, wo
 
         tab_codes = keep.tile([P, T], I32, name="tab_codes", align_bytes=64)
         nc.sync.dma_start(tab_codes[:], tab_words[0].rearrange("p n t -> p (n t)").bitcast(I32))
+        temper_col = keep.tile([P, 1], F32, name="temper_col")
+        nc.sync.dma_start(temper_col[:], temper)
         wo_raw = keep.tile([P, PACK * R], F32, name="wo_raw", tag="wo_then_p1")
         nc.sync.dma_start(wo_raw[:], wo.rearrange("(p t) r -> p (t r)", t=PACK))
         dy_raw = keep.tile([P, PACK * M], F32, name="dy_raw", tag="dy_then_s")
@@ -54,19 +58,11 @@ def tile_attend_cpickshares_kernel(tc, tab_words, tab_scales, w1, temper, pw, wo
         old_sb = keep.tile([P, J], F32, name="old_sb")
         nc.sync.dma_start(old_sb[:], old)
 
-        pw_pairs = keep.tile([P, 2], F32, name="pw_pairs")
-        nc.gpsimd.dma_start(pw_pairs[:], pw.rearrange("o (p c) -> (o p) c", c=2))
-        temper_col = keep.tile([P, 1], F32, name="temper_col")
-        nc.gpsimd.dma_start(temper_col[:], temper)
         ident = keep.tile([P, P], F32, name="ident")
         make_identity(nc, ident[:])
         placed = keep.tile([P, J], F32, name="placed")
         nc.vector.memset(placed[:], 0.0)
 
-        warm = keep.tile([P, 1], F32, name="warm")
-        nc.vector.memset(warm[:], 1.0)
-        warm_exp = keep.tile([P, 1], F32, name="warm_exp")
-        nc.scalar.activation(warm_exp[:], warm[:], ACT.Exp)
 
         w1_bf = keep.tile([P, R * PACK], BF16, name="w1_bf", align_bytes=64)
         nc.vector.tensor_copy(w1_bf[:].rearrange("p (r t) -> p r t", t=PACK), w1_raw[:].rearrange("p (t r) -> p r t", t=PACK))
@@ -77,35 +73,44 @@ def tile_attend_cpickshares_kernel(tc, tab_words, tab_scales, w1, temper, pw, wo
         w1_codes = keep.tile([P, R], U32, name="w1_codes", align_bytes=64)
         w1_plane = keep.tile([P, R], U8, name="w1_plane", align_bytes=64)
         nc.vector.quantize_mx(w1_codes[:].bitcast(FP8X4), w1_plane[:], w1_bf[:])
-        neg_temper = keep.tile([P, 1], F32, name="neg_temper")
-        nc.gpsimd.tensor_scalar(neg_temper[:], temper_col[:], -1.0, 0.0, ALU.mult, ALU.add)
 
         pw_ps = psum.tile([P, 2, P], F32, name="pw_ps")
         for c in range(2):
             nc.tensor.transpose(pw_ps[:, c, :], pw_pairs[:, c : c + 1].to_broadcast([P, P]), ident[:])
         pw_row = keep.tile([P, M], F32, name="pw_row")
-        nc.scalar.copy(pw_row[:].rearrange("p (q c) -> p q c", c=2), pw_ps[:].rearrange("p c q -> p q c"))
+        nc.scalar.activation(pw_row[:].rearrange("p (q c) -> p q c", c=2), pw_ps[:].rearrange("p c q -> p q c"), ACT.Copy)
 
         wo_bf = keep.tile([P, R * PACK], BF16, name="wo_bf", align_bytes=64)
-        nc.scalar.copy(wo_bf[:].rearrange("p (r t) -> p r t", t=PACK), wo_raw[:].rearrange("p (t r) -> p r t", t=PACK))
+        nc.scalar.activation(wo_bf[:].rearrange("p (r t) -> p r t", t=PACK), wo_raw[:].rearrange("p (t r) -> p r t", t=PACK), ACT.Copy, scale=-1.0)
 
         p1 = keep.tile([P, J], F32, name="p1", tag="wo_then_p1")
         for h in range(HALVES):
             cols = slice(h * jh, (h + 1) * jh)
             got_codes = keep.tile([P, jh], U32, name="got_codes%d" % h, align_bytes=64)
             nc.vector.tensor_copy(got_codes[:], tab_codes[:].bitcast(U32).indirect(slots[:, h * jh // 16 : (h + 1) * jh // 16]))
-            a_ps = psum.tile([P, jh], F32, name="a_ps%d" % h)
-            nc.tensor.matmul_mx(a_ps[:], lhsT=w1_codes[:].bitcast(FP8X4), lhsT_scale=w1_plane[:],
-                                rhs=got_codes[:].bitcast(FP8X4), rhs_scale=got_plane[:, cols], start=True, stop=True)
-            nc.scalar.activation(p1[:, cols], a_ps[:], ACT.Exp, scale=temper_col[:])
-        warm_ars = keep.tile([P, 1], F32, name="warm_ars")
-        nc.scalar.activation(warm_ars[:], p1[:, J - 1 : J], ACT.Abs_reciprocal_sqrt)
+            width = jh // (h + 1)
+            for c in range(h + 1):
+                part = slice(h * jh + c * width, h * jh + (c + 1) * width)
+                a_ps = psum.tile([P, width], F32, name="a_ps%d_%d" % (h, c))
+                nc.tensor.matmul_mx(a_ps[:], lhsT=w1_codes[:].bitcast(FP8X4), lhsT_scale=w1_plane[:],
+                                    rhs=got_codes[:, c * width : (c + 1) * width].bitcast(FP8X4), rhs_scale=got_plane[:, part], start=True, stop=True)
+                nc.scalar.activation(p1[:, part], a_ps[:], ACT.Exp, scale=temper_col[:])
 
         wo_codes = keep.tile([P, R], U32, name="wo_codes", align_bytes=64)
         wo_plane = keep.tile([P, R], U8, name="wo_plane", align_bytes=64)
         nc.vector.quantize_mx(wo_codes[:].bitcast(FP8X4), wo_plane[:], wo_bf[:])
-        dy_bf = keep.tile([P, M * PACK], BF16, name="dy_bf", align_bytes=64)
-        nc.vector.tensor_copy(dy_bf[:].rearrange("p (m t) -> p m t", t=PACK), dy_raw[:].rearrange("p (t m) -> p m t", t=PACK))
+        dy_codes = keep.tile([P, M], U32, name="dy_codes", align_bytes=64)
+        dy_plane = keep.tile([P, M], U8, name="dy_plane", align_bytes=64)
+        dy_rows = dy_raw[:].rearrange("p (t m) -> p m t", t=PACK)
+        dy_bf = [keep.tile([P, mh * PACK], BF16, name="dy_bf%d" % h, align_bytes=64) for h in range(HALVES)]
+        for h in range(HALVES):
+            nc.vector.tensor_copy(dy_bf[h][:].rearrange("p (m t) -> p m t", t=PACK), dy_rows[:, h * mh : (h + 1) * mh, :])
+
+        def quantise_dy(h):
+            cols = slice(h * mh, (h + 1) * mh)
+            nc.vector.quantize_mx(dy_codes[:, cols].bitcast(FP8X4), dy_plane[:, cols], dy_bf[h][:])
+
+        quantise_dy(0)
 
         def half_tiles(name, width):
             return [keep.tile([P, width], F32, name="%s%d" % (name, h)) for h in range(HALVES)]
@@ -126,9 +131,11 @@ def tile_attend_cpickshares_kernel(tc, tab_words, tab_scales, w1, temper, pw, wo
         share = half_tiles("share", mh)
         root = half_tiles("root", mh)
         inv = half_tiles("inv", mh)
-        wn = half_tiles("wn", mh)
+        wn_both = keep.tile([P, M], F32, name="wn_both")
+        wn = [wn_both[:, h * mh : (h + 1) * mh] for h in range(HALVES)]
         wsum = half_tiles("wsum", gh)
-        back = half_tiles("back", mh)
+        back_both = keep.tile([P, M], F32, name="back_both")
+        back = [back_both[:, h * mh : (h + 1) * mh] for h in range(HALVES)]
         both = range(HALVES)
 
         for h in both:
@@ -144,9 +151,7 @@ def tile_attend_cpickshares_kernel(tc, tab_words, tab_scales, w1, temper, pw, wo
         for h in both:
             nc.scalar.activation(inv[h][:], root[h][:], ACT.Square)
 
-        dy_codes = keep.tile([P, M], U32, name="dy_codes", align_bytes=64)
-        dy_plane = keep.tile([P, M], U8, name="dy_plane", align_bytes=64)
-        nc.vector.quantize_mx(dy_codes[:].bitcast(FP8X4), dy_plane[:], dy_bf[:])
+        quantise_dy(1)
         c0 = psum.tile([P, M], F32, name="c0")
         nc.tensor.matmul_mx(c0[:], lhsT=wo_codes[:].bitcast(FP8X4), lhsT_scale=wo_plane[:],
                             rhs=dy_codes[:].bitcast(FP8X4), rhs_scale=dy_plane[:], start=True, stop=True)
@@ -157,12 +162,11 @@ def tile_attend_cpickshares_kernel(tc, tab_words, tab_scales, w1, temper, pw, wo
             nc.vector.tensor_reduce(wsum[h][:], grouped(wn[h]), AX.X, ALU.add)
         for h in both:
             nc.vector.scalar_tensor_tensor(grouped(back[h]), grouped(share[h]), -1.0, spread(wsum[h]), ALU.mult, ALU.mult)
-        for h in both:
-            nc.vector.tensor_tensor(placed[:].indirect(pick_list(h)), wn[h][:], back[h][:], ALU.add)
+        nc.vector.tensor_tensor(placed[:].indirect(picks[:]), wn_both[:], back_both[:], ALU.add)
 
         queues = (nc.sync, nc.scalar)
         for h in both:
             cols = slice(h * jh, (h + 1) * jh)
             result = keep.tile([P, jh], F32, name="result%d" % h)
-            nc.vector.scalar_tensor_tensor(result[:], placed[:, cols], neg_temper[:], old_sb[:, cols], ALU.mult, ALU.add)
+            nc.vector.scalar_tensor_tensor(result[:], placed[:, cols], temper_col[:], old_sb[:, cols], ALU.mult, ALU.add)
             queues[h].dma_start(out[:, cols], result[:])

from contextlib import ExitStack

import concourse.mybir as mybir
from concourse.masks import make_identity

K, R, F, T, J, M, G = 512, 128, 512, 2048, 512, 256, 32
FLOPS = 2 * K * R * J + 2 * F * R * M

F32 = mybir.dt.float32
BF16 = mybir.dt.bfloat16
I32 = mybir.dt.int32
U32 = mybir.dt.uint32
U16 = mybir.dt.uint16
U8 = mybir.dt.uint8
FP8X4 = mybir.dt.float8_e4m3fn_x4
ALU = mybir.AluOpType
ACT = mybir.ActivationFunctionType
AX = mybir.AxisListType

P = 128
PACK = 4
GROUP = M // G
HALVES = 2


def tile_attend_cpickshares_kernel(tc, tab_words, tab_scales, w1, temper, pw, wo, dy, old, offs, offs2, out):
    nc = tc.nc
    jh = J // HALVES
    mh = M // HALVES
    gh = G // HALVES
    with ExitStack() as ctx:
        keep = ctx.enter_context(tc.tile_pool(name="keep", bufs=1))
        psum = ctx.enter_context(tc.psum_pool(name="psum", bufs=1))

        slots = keep.tile([P, J // 16], U16, name="slots")
        nc.sync.dma_start(slots[:], offs)

        w1_raw = keep.tile([P, PACK * R], F32, name="w1_raw", align_bytes=64)
        nc.sync.dma_start(w1_raw[:], w1.rearrange("(p t) r -> p (t r)", t=PACK))
        pw_pairs = keep.tile([P, 2], F32, name="pw_pairs")
        nc.sync.dma_start(pw_pairs[:], pw.rearrange("o (p c) -> (o p) c", c=2))
        tab_plane = keep.tile([P, T], U8, name="tab_plane", align_bytes=64)
        nc.vector.memset(tab_plane[:].bitcast(I32), 0)
        scale_rows = tab_scales[0].bitcast(I32)
        for i in range(PACK):
            nc.sync.dma_start(tab_plane[:].bitcast(I32)[i:P:32, :], scale_rows[i:16:PACK, :])

        tab_codes = keep.tile([P, T], I32, name="tab_codes", align_bytes=64)
        nc.sync.dma_start(tab_codes[:], tab_words[0].rearrange("p n t -> p (n t)").bitcast(I32))
        temper_col = keep.tile([P, 1], F32, name="temper_col")
        nc.sync.dma_start(temper_col[:], temper)
        wo_raw = keep.tile([P, PACK * R], F32, name="wo_raw", tag="wo_then_p1")
        nc.sync.dma_start(wo_raw[:], wo.rearrange("(p t) r -> p (t r)", t=PACK))
        dy_raw = keep.tile([P, PACK * M], F32, name="dy_raw", tag="dy_then_s")
        nc.sync.dma_start(dy_raw[:], dy.rearrange("(p t) m -> p (t m)", t=PACK))
        picks = keep.tile([P, M // 16], U16, name="picks")
        nc.sync.dma_start(picks[:], offs2)
        old_sb = keep.tile([P, J], F32, name="old_sb")
        nc.sync.dma_start(old_sb[:], old)

        ident = keep.tile([P, P], F32, name="ident")
        make_identity(nc, ident[:])
        placed = keep.tile([P, J], F32, name="placed")
        nc.vector.memset(placed[:], 0.0)


        w1_bf = keep.tile([P, R * PACK], BF16, name="w1_bf", align_bytes=64)
        nc.vector.tensor_copy(w1_bf[:].rearrange("p (r t) -> p r t", t=PACK), w1_raw[:].rearrange("p (t r) -> p r t", t=PACK))


        got_plane = keep.tile([P, J], U8, name="got_plane", align_bytes=64)
        nc.vector.tensor_copy(got_plane[:], tab_plane[:].indirect(slots[:]))
        w1_codes = keep.tile([P, R], U32, name="w1_codes", align_bytes=64)
        w1_plane = keep.tile([P, R], U8, name="w1_plane", align_bytes=64)
        nc.vector.quantize_mx(w1_codes[:].bitcast(FP8X4), w1_plane[:], w1_bf[:])

        pw_ps = psum.tile([P, 2, P], F32, name="pw_ps")
        for c in range(2):
            nc.tensor.transpose(pw_ps[:, c, :], pw_pairs[:, c : c + 1].to_broadcast([P, P]), ident[:])
        pw_row = keep.tile([P, M], F32, name="pw_row")
        nc.scalar.activation(pw_row[:].rearrange("p (q c) -> p q c", c=2), pw_ps[:].rearrange("p c q -> p q c"), ACT.Copy)

        wo_bf = keep.tile([P, R * PACK], BF16, name="wo_bf", align_bytes=64)
        nc.scalar.activation(wo_bf[:].rearrange("p (r t) -> p r t", t=PACK), wo_raw[:].rearrange("p (t r) -> p r t", t=PACK), ACT.Copy, scale=-1.0)

        p1 = keep.tile([P, J], F32, name="p1", tag="wo_then_p1")
        for h in range(HALVES):
            cols = slice(h * jh, (h + 1) * jh)
            got_codes = keep.tile([P, jh], U32, name="got_codes%d" % h, align_bytes=64)
            nc.vector.tensor_copy(got_codes[:], tab_codes[:].bitcast(U32).indirect(slots[:, h * jh // 16 : (h + 1) * jh // 16]))
            width = jh // (h + 1)
            for c in range(h + 1):
                part = slice(h * jh + c * width, h * jh + (c + 1) * width)
                a_ps = psum.tile([P, width], F32, name="a_ps%d_%d" % (h, c))
                nc.tensor.matmul_mx(a_ps[:], lhsT=w1_codes[:].bitcast(FP8X4), lhsT_scale=w1_plane[:],
                                    rhs=got_codes[:, c * width : (c + 1) * width].bitcast(FP8X4), rhs_scale=got_plane[:, part], start=True, stop=True)
                nc.scalar.activation(p1[:, part], a_ps[:], ACT.Exp, scale=temper_col[:])

        wo_codes = keep.tile([P, R], U32, name="wo_codes", align_bytes=64)
        wo_plane = keep.tile([P, R], U8, name="wo_plane", align_bytes=64)
        nc.vector.quantize_mx(wo_codes[:].bitcast(FP8X4), wo_plane[:], wo_bf[:])
        dy_codes = keep.tile([P, M], U32, name="dy_codes", align_bytes=64)
        dy_plane = keep.tile([P, M], U8, name="dy_plane", align_bytes=64)
        dy_rows = dy_raw[:].rearrange("p (t m) -> p m t", t=PACK)
        dy_bf = [keep.tile([P, mh * PACK], BF16, name="dy_bf%d" % h, align_bytes=64) for h in range(HALVES)]
        for h in range(HALVES):
            nc.vector.tensor_copy(dy_bf[h][:].rearrange("p (m t) -> p m t", t=PACK), dy_rows[:, h * mh : (h + 1) * mh, :])

        def quantise_dy(h):
            cols = slice(h * mh, (h + 1) * mh)
            nc.vector.quantize_mx(dy_codes[:, cols].bitcast(FP8X4), dy_plane[:, cols], dy_bf[h][:])

        quantise_dy(0)

        def half_tiles(name, width):
            return [keep.tile([P, width], F32, name="%s%d" % (name, h)) for h in range(HALVES)]

        def grouped(tile):
            return tile[:].rearrange("p (g e) -> p g e", e=GROUP)

        def spread(tile):
            return tile[:].unsqueeze(2).to_broadcast([P, gh, GROUP])

        def pick_list(h):
            return picks[:, h * mh // 16 : (h + 1) * mh // 16]

        s_both = keep.tile([P, M], F32, name="s_both", tag="dy_then_s")
        s = [s_both[:, h * mh : (h + 1) * mh] for h in range(HALVES)]
        z = half_tiles("z", gh)
        rz = half_tiles("rz", gh)
        share = half_tiles("share", mh)
        root = half_tiles("root", mh)
        inv = half_tiles("inv", mh)
        wn_both = keep.tile([P, M], F32, name="wn_both")
        wn = [wn_both[:, h * mh : (h + 1) * mh] for h in range(HALVES)]
        wsum = half_tiles("wsum", gh)
        back_both = keep.tile([P, M], F32, name="back_both")
        back = [back_both[:, h * mh : (h + 1) * mh] for h in range(HALVES)]
        both = range(HALVES)

        for h in both:
            nc.vector.tensor_tensor(s[h][:], p1[:].indirect(pick_list(h)), pw_row[:, h * mh : (h + 1) * mh], ALU.mult)
        for h in both:
            nc.vector.tensor_reduce(z[h][:], grouped(s[h]), AX.X, ALU.add)
        for h in both:
            nc.vector.reciprocal(rz[h][:], z[h][:])
        for h in both:
            nc.vector.tensor_tensor(grouped(share[h]), grouped(s[h]), spread(rz[h]), ALU.mult)
        for h in both:
            nc.scalar.activation(root[h][:], share[h][:], ACT.Abs_reciprocal_sqrt, bias=1.0, scale=8.0)
        for h in both:
            nc.scalar.activation(inv[h][:], root[h][:], ACT.Square)

        quantise_dy(1)
        c0 = psum.tile([P, M], F32, name="c0")
        nc.tensor.matmul_mx(c0[:], lhsT=wo_codes[:].bitcast(FP8X4), lhsT_scale=wo_plane[:],
                            rhs=dy_codes[:].bitcast(FP8X4), rhs_scale=dy_plane[:], start=True, stop=True)

        for h in both:
            nc.vector.scalar_tensor_tensor(wn[h][:], inv[h][:], 1.0, c0[:, h * mh : (h + 1) * mh], ALU.subtract, ALU.mult)
        for h in both:
            nc.vector.tensor_reduce(wsum[h][:], grouped(wn[h]), AX.X, ALU.add)
        for h in both:
            nc.vector.scalar_tensor_tensor(grouped(back[h]), grouped(share[h]), -1.0, spread(wsum[h]), ALU.mult, ALU.mult)
        nc.vector.tensor_tensor(placed[:].indirect(picks[:]), wn_both[:], back_both[:], ALU.add)

        queues = (nc.sync, nc.scalar)
        for h in both:
            cols = slice(h * jh, (h + 1) * jh)
            result = keep.tile([P, jh], F32, name="result%d" % h)
            nc.vector.scalar_tensor_tensor(result[:], placed[:, cols], temper_col[:], old_sb[:, cols], ALU.mult, ALU.add)
            queues[h].dma_start(out[:, cols], result[:])
